import numpy as np
import ml_dtypes

BF16 = ml_dtypes.bfloat16


def bf(x):
    return np.asarray(x, np.float32).astype(BF16)


def f32(x):
    return np.asarray(x, np.float32)


def f64(x):
    return np.asarray(x).astype(np.float64)


def striped(idx):
    return np.tile(idx.reshape(-1, 16).T, (8, 1))


def rows(idx, k):
    return np.tile(idx, (k, 1))


def look(tab, idx):
    return np.take_along_axis(f64(tab), rows(idx, len(tab)), axis=1)


K, S, V, N, M = 128, 2048, 1024, 1024, 256


def setup_inputs():
    return {"tab": f32(np.random.standard_normal((2, K, S))), "w": bf(np.random.standard_normal((K, M)) / np.sqrt(K)), "offs": striped(np.random.permutation(S)[:N])}


def reference(tab, w, offs):
    idx = offs[:16].T.reshape(-1)
    x = 1.0 / (1.0 + np.exp(-look(tab[0], idx))) * np.tanh(look(tab[1], idx))
    y = f64(w).T @ x
    return y

@@ -1,0 +1,52 @@
+import concourse.mybir as mybir
+
+P = 128
+PLACES = 2048
+N = 1024
+M = 256
+PIECE = 512
+COLUMNS = PIECE // 16
+
+F32 = mybir.dt.float32
+BF16 = mybir.dt.bfloat16
+U16 = mybir.dt.uint16
+SIGMOID = mybir.ActivationFunctionType.Sigmoid
+TANH = mybir.ActivationFunctionType.Tanh
+MULT = mybir.AluOpType.mult
+
+FLOPS = 2 * P * M * N
+
+
+def tile_lookup_cell_sigtanh_none_kernel(tc, tab, w, offs, out):
+    nc = tc.nc
+    with (
+        tc.tile_pool(name="held", bufs=1) as held,
+        tc.tile_pool(name="work", bufs=2) as work,
+        tc.psum_pool(name="psum", bufs=2) as psum,
+    ):
+        offsets = held.tile([P, N // 16], U16, name="offsets")
+        gate_table = held.tile([P, PLACES], F32, name="gate_table")
+        state_table = held.tile([P, PLACES], F32, name="state_table")
+        weights = held.tile([P, M], BF16, name="weights")
+        nc.sync.dma_start(offsets[:], offs)
+        nc.sync.dma_start(gate_table[:], tab[0])
+        nc.sync.dma_start(state_table[:], tab[1])
+        nc.sync.dma_start(weights[:], w)
+
+        gates = held.tile([P, N], F32, name="gates")
+        for j in range(0, N, PIECE):
+            piece_offsets = offsets[:, j // 16 : j // 16 + COLUMNS]
+            nc.scalar.activation(gates[:, j : j + PIECE], gate_table[:].indirect(piece_offsets), SIGMOID)
+
+        for j in range(0, N, PIECE):
+            piece_offsets = offsets[:, j // 16 : j // 16 + COLUMNS]
+            state = work.tile([P, PIECE], F32, name="state")
+            nc.scalar.activation(state[:], state_table[:].indirect(piece_offsets), TANH)
+            x = work.tile([P, PIECE], BF16, name="x")
+            nc.vector.tensor_tensor(x[:], gates[:, j : j + PIECE], state[:], MULT)
+            for m in range(0, M, P):
+                product = psum.tile([P, PIECE], F32, name="product")
+                nc.tensor.matmul(product[:], weights[:, m : m + P], x[:], start=True, stop=True)
+                result = work.tile([P, PIECE], F32, name="result")
+                nc.vector.tensor_copy(result[:], product[:])
+                nc.sync.dma_start(out[m : m + P, j : j + PIECE], result[:])

@@ -5,7 +5,7 @@ PLACES = 2048
 N = 1024
 M = 256
 PIECE = 512
-COLUMNS = PIECE // 16
+STATE_PIECE = 256
 
 F32 = mybir.dt.float32
 BF16 = mybir.dt.bfloat16
@@ -21,8 +21,8 @@ def tile_lookup_cell_sigtanh_none_kernel(tc, tab, w, offs, out):
     nc = tc.nc
     with (
         tc.tile_pool(name="held", bufs=1) as held,
-        tc.tile_pool(name="work", bufs=2) as work,
-        tc.psum_pool(name="psum", bufs=2) as psum,
+        tc.tile_pool(name="work", bufs=N // STATE_PIECE) as work,
+        tc.psum_pool(name="psum", bufs=N // STATE_PIECE) as psum,
     ):
         offsets = held.tile([P, N // 16], U16, name="offsets")
         gate_table = held.tile([P, PLACES], F32, name="gate_table")
@@ -33,20 +33,34 @@ def tile_lookup_cell_sigtanh_none_kernel(tc, tab, w, offs, out):
         nc.sync.dma_start(state_table[:], tab[1])
         nc.sync.dma_start(weights[:], w)
 
+        zeros = held.tile([P, 1], F32, name="zeros")
+        warm = held.tile([P, 1], F32, name="warm")
+        nc.vector.memset(zeros[:], 0.0)
+        nc.scalar.activation(warm[:], zeros[:], SIGMOID)
+
         gates = held.tile([P, N], F32, name="gates")
         for j in range(0, N, PIECE):
-            piece_offsets = offsets[:, j // 16 : j // 16 + COLUMNS]
+            piece_offsets = offsets[:, j // 16 : (j + PIECE) // 16]
             nc.scalar.activation(gates[:, j : j + PIECE], gate_table[:].indirect(piece_offsets), SIGMOID)
 
-        for j in range(0, N, PIECE):
-            piece_offsets = offsets[:, j // 16 : j // 16 + COLUMNS]
-            state = work.tile([P, PIECE], F32, name="state")
+        xs = []
+        for j in range(0, N, STATE_PIECE):
+            piece_offsets = offsets[:, j // 16 : (j + STATE_PIECE) // 16]
+            state = work.tile([P, STATE_PIECE], F32, name="state")
             nc.scalar.activation(state[:], state_table[:].indirect(piece_offsets), TANH)
-            x = work.tile([P, PIECE], BF16, name="x")
-            nc.vector.tensor_tensor(x[:], gates[:, j : j + PIECE], state[:], MULT)
-            for m in range(0, M, P):
-                product = psum.tile([P, PIECE], F32, name="product")
-                nc.tensor.matmul(product[:], weights[:, m : m + P], x[:], start=True, stop=True)
-                result = work.tile([P, PIECE], F32, name="result")
-                nc.vector.tensor_copy(result[:], product[:])
-                nc.sync.dma_start(out[m : m + P, j : j + PIECE], result[:])
+            x = work.tile([P, STATE_PIECE], BF16, name="x")
+            nc.vector.tensor_tensor(x[:], gates[:, j : j + STATE_PIECE], state[:], MULT)
+            xs.append(x)
+
+        for i, x in enumerate(xs):
+            j = i * STATE_PIECE
+            upper = psum.tile([P, STATE_PIECE], F32, name="upper")
+            lower = psum.tile([P, STATE_PIECE], F32, name="lower")
+            nc.tensor.matmul(upper[:], weights[:, 0:P], x[:], start=True, stop=True)
+            nc.tensor.matmul(lower[:], weights[:, P:M], x[:], start=True, stop=True)
+            upper_out = work.tile([P, STATE_PIECE], F32, name="upper_out")
+            lower_out = work.tile([P, STATE_PIECE], F32, name="lower_out")
+            nc.vector.tensor_copy(upper_out[:], upper[:])
+            nc.scalar.copy(lower_out[:], lower[:])
+            nc.sync.dma_start(out[0:P, j : j + STATE_PIECE], upper_out[:])
+            nc.sync.dma_start(out[P:M, j : j + STATE_PIECE], lower_out[:])

@@ -52,15 +52,14 @@ def tile_lookup_cell_sigtanh_none_kernel(tc, tab, w, offs, out):
             nc.vector.tensor_tensor(x[:], gates[:, j : j + STATE_PIECE], state[:], MULT)
             xs.append(x)
 
+        out_halves = out.rearrange("(h p) j -> p h j", p=P)
         for i, x in enumerate(xs):
             j = i * STATE_PIECE
             upper = psum.tile([P, STATE_PIECE], F32, name="upper")
             lower = psum.tile([P, STATE_PIECE], F32, name="lower")
             nc.tensor.matmul(upper[:], weights[:, 0:P], x[:], start=True, stop=True)
             nc.tensor.matmul(lower[:], weights[:, P:M], x[:], start=True, stop=True)
-            upper_out = work.tile([P, STATE_PIECE], F32, name="upper_out")
-            lower_out = work.tile([P, STATE_PIECE], F32, name="lower_out")
-            nc.vector.tensor_copy(upper_out[:], upper[:])
-            nc.scalar.copy(lower_out[:], lower[:])
-            nc.sync.dma_start(out[0:P, j : j + STATE_PIECE], upper_out[:])
-            nc.sync.dma_start(out[P:M, j : j + STATE_PIECE], lower_out[:])
+            results = work.tile([P, 2, STATE_PIECE], F32, name="results")
+            nc.vector.tensor_copy(results[:, 0, :], upper[:])
+            nc.scalar.copy(results[:, 1, :], lower[:])
+            nc.sync.dma_start(out_halves[:, :, j : j + STATE_PIECE], results[:])

@@ -4,8 +4,7 @@ P = 128
 PLACES = 2048
 N = 1024
 M = 256
-PIECE = 512
-STATE_PIECE = 256
+PIECE = 256
 
 F32 = mybir.dt.float32
 BF16 = mybir.dt.bfloat16
@@ -21,8 +20,8 @@ def tile_lookup_cell_sigtanh_none_kernel(tc, tab, w, offs, out):
     nc = tc.nc
     with (
         tc.tile_pool(name="held", bufs=1) as held,
-        tc.tile_pool(name="work", bufs=N // STATE_PIECE) as work,
-        tc.psum_pool(name="psum", bufs=N // STATE_PIECE) as psum,
+        tc.tile_pool(name="work", bufs=N // PIECE) as work,
+        tc.psum_pool(name="psum", bufs=N // PIECE) as psum,
     ):
         offsets = held.tile([P, N // 16], U16, name="offsets")
         gate_table = held.tile([P, PLACES], F32, name="gate_table")
@@ -39,27 +38,25 @@ def tile_lookup_cell_sigtanh_none_kernel(tc, tab, w, offs, out):
         nc.scalar.activation(warm[:], zeros[:], SIGMOID)
 
         gates = held.tile([P, N], F32, name="gates")
-        for j in range(0, N, PIECE):
-            piece_offsets = offsets[:, j // 16 : (j + PIECE) // 16]
-            nc.scalar.activation(gates[:, j : j + PIECE], gate_table[:].indirect(piece_offsets), SIGMOID)
+        nc.scalar.activation(gates[:], gate_table[:].indirect(offsets[:]), SIGMOID)
 
         xs = []
-        for j in range(0, N, STATE_PIECE):
-            piece_offsets = offsets[:, j // 16 : (j + STATE_PIECE) // 16]
-            state = work.tile([P, STATE_PIECE], F32, name="state")
+        for j in range(0, N, PIECE):
+            piece_offsets = offsets[:, j // 16 : (j + PIECE) // 16]
+            state = work.tile([P, PIECE], F32, name="state")
             nc.scalar.activation(state[:], state_table[:].indirect(piece_offsets), TANH)
-            x = work.tile([P, STATE_PIECE], BF16, name="x")
-            nc.vector.tensor_tensor(x[:], gates[:, j : j + STATE_PIECE], state[:], MULT)
+            x = work.tile([P, PIECE], BF16, name="x")
+            nc.vector.tensor_tensor(x[:], gates[:, j : j + PIECE], state[:], MULT)
             xs.append(x)
 
         out_halves = out.rearrange("(h p) j -> p h j", p=P)
         for i, x in enumerate(xs):
-            j = i * STATE_PIECE
-            upper = psum.tile([P, STATE_PIECE], F32, name="upper")
-            lower = psum.tile([P, STATE_PIECE], F32, name="lower")
+            j = i * PIECE
+            upper = psum.tile([P, PIECE], F32, name="upper")
+            lower = psum.tile([P, PIECE], F32, name="lower")
             nc.tensor.matmul(upper[:], weights[:, 0:P], x[:], start=True, stop=True)
             nc.tensor.matmul(lower[:], weights[:, P:M], x[:], start=True, stop=True)
-            results = work.tile([P, 2, STATE_PIECE], F32, name="results")
+            results = work.tile([P, 2, PIECE], F32, name="results")
             nc.vector.tensor_copy(results[:, 0, :], upper[:])
             nc.scalar.copy(results[:, 1, :], lower[:])
-            nc.sync.dma_start(out_halves[:, :, j : j + STATE_PIECE], results[:])
+            nc.sync.dma_start(out_halves[:, :, j : j + PIECE], results[:])

import concourse.mybir as mybir

P = 128
PLACES = 2048
N = 1024
M = 256
PIECE = 256

F32 = mybir.dt.float32
BF16 = mybir.dt.bfloat16
U16 = mybir.dt.uint16
SIGMOID = mybir.ActivationFunctionType.Sigmoid
TANH = mybir.ActivationFunctionType.Tanh
MULT = mybir.AluOpType.mult

FLOPS = 2 * P * M * N


def tile_lookup_cell_sigtanh_none_kernel(tc, tab, w, offs, out):
    nc = tc.nc
    with (
        tc.tile_pool(name="held", bufs=1) as held,
        tc.tile_pool(name="work", bufs=N // PIECE) as work,
        tc.psum_pool(name="psum", bufs=N // PIECE) as psum,
    ):
        offsets = held.tile([P, N // 16], U16, name="offsets")
        gate_table = held.tile([P, PLACES], F32, name="gate_table")
        state_table = held.tile([P, PLACES], F32, name="state_table")
        weights = held.tile([P, M], BF16, name="weights")
        nc.sync.dma_start(offsets[:], offs)
        nc.sync.dma_start(gate_table[:], tab[0])
        nc.sync.dma_start(state_table[:], tab[1])
        nc.sync.dma_start(weights[:], w)

        zeros = held.tile([P, 1], F32, name="zeros")
        warm = held.tile([P, 1], F32, name="warm")
        nc.vector.memset(zeros[:], 0.0)
        nc.scalar.activation(warm[:], zeros[:], SIGMOID)

        gates = held.tile([P, N], F32, name="gates")
        nc.scalar.activation(gates[:], gate_table[:].indirect(offsets[:]), SIGMOID)

        xs = []
        for j in range(0, N, PIECE):
            piece_offsets = offsets[:, j // 16 : (j + PIECE) // 16]
            state = work.tile([P, PIECE], F32, name="state")
            nc.scalar.activation(state[:], state_table[:].indirect(piece_offsets), TANH)
            x = work.tile([P, PIECE], BF16, name="x")
            nc.vector.tensor_tensor(x[:], gates[:, j : j + PIECE], state[:], MULT)
            xs.append(x)

        out_halves = out.rearrange("(h p) j -> p h j", p=P)
        for i, x in enumerate(xs):
            j = i * PIECE
            upper = psum.tile([P, PIECE], F32, name="upper")
            lower = psum.tile([P, PIECE], F32, name="lower")
            nc.tensor.matmul(upper[:], weights[:, 0:P], x[:], start=True, stop=True)
            nc.tensor.matmul(lower[:], weights[:, P:M], x[:], start=True, stop=True)
            results = work.tile([P, 2, PIECE], F32, name="results")
            nc.vector.tensor_copy(results[:, 0, :], upper[:])
            nc.scalar.copy(results[:, 1, :], lower[:])
            nc.sync.dma_start(out_halves[:, :, j : j + PIECE], results[:])
